import numpy as np
import ml_dtypes


def mxq(x, axis, fmt="e4m3"):
    dtype, down = {"e4m3": (ml_dtypes.float8_e4m3fn, 7), "e5m2": (ml_dtypes.float8_e5m2, 14)}[fmt]
    v = np.moveaxis(np.asarray(x, np.float32).astype(ml_dtypes.bfloat16).astype(np.float64), axis, -1)
    blocks = v.reshape(v.shape[:-1] + (-1, 32))
    amax = np.abs(blocks).max(-1, keepdims=True)
    byte = np.maximum(np.where(amax > 0, np.frexp(amax)[1] - 1 + 127, 0) - down, 1)
    scale = np.exp2(byte - 127.0)
    codes = (blocks / scale).astype(np.float32).astype(dtype).astype(np.float64)
    return np.moveaxis((codes * scale).reshape(v.shape), -1, axis)


WIDE = False


def mx_kscale(k):
    if not WIDE:
        return np.ones(k)
    levels = np.array([10, -10, 5, -5, 0])
    if k % 512:
        return np.exp2(np.random.permutation(np.resize(levels, k // 32))).repeat(32)
    a = np.empty((k // 512, 16))
    for p in range(k // 512):
        a[p, :8] = np.random.permutation(np.resize(levels, 8))
        for g in range(8):
            far = levels[np.abs(levels - a[p, g]) >= 10]
            a[p, g + 8] = far[np.random.randint(len(far))]
    return np.exp2(a.ravel()).repeat(32)


def f64(x):
    return np.asarray(x).astype(np.float64)


def striped8(idx):
    return np.asarray(idx).reshape(8, -1, 16).transpose(0, 2, 1).reshape(128, -1).astype(np.uint16)


def unstriped8(offs):
    return offs.reshape(8, 16, -1).transpose(0, 2, 1).reshape(8, -1).astype(np.int64)


def pick8(x, idx, run):
    r = np.arange(len(x))
    return x[r[:, None], idx[r % (8 * run) // run]]


E2M1 = np.array([0.0, 0.5, 1.0, 1.5, 2.0, 3.0, 4.0, 6.0, -0.0, -0.5, -1.0, -1.5, -2.0, -3.0, -4.0, -6.0])


def pack_weight(w, fmt):
    k, n = w.shape
    w = f64(np.asarray(w, np.float32).astype(ml_dtypes.bfloat16)).reshape(k // 32, 32, n)
    amax = np.abs(w).max(1)
    if fmt == "e4m3":
        byte = np.frexp(amax)[1] - 1 + 127 - 7
    else:
        mant, ex = np.frexp(amax / 6.0)
        byte = np.where(mant > 0.5, ex, ex - 1) + 127
    byte = np.clip(np.where(amax > 0, byte, 1), 1, 254)
    scaled = (w * np.exp2(127.0 - byte)[:, None, :]).reshape(k, n).astype(np.float32)
    by_word = np.ascontiguousarray(scaled.reshape(k // 512, 128, 4, n).transpose(0, 1, 3, 2))
    if fmt == "e4m3":
        words = by_word.astype(ml_dtypes.float8_e4m3fn).view(np.uint8)
    else:
        c = by_word.astype(ml_dtypes.float4_e2m1fn).view(np.uint8) & 0xF
        words = (c[..., 0::2] | (c[..., 1::2] << 4)).reshape(k // 512, 128, 2 * n)
    return np.ascontiguousarray(words), np.ascontiguousarray(byte.astype(np.uint8).reshape(k // 512, 16, n))


def unpack_weight(words, scales, fmt):
    g, _, n = scales.shape
    words = np.ascontiguousarray(words).reshape(g, 128, n, -1)
    if fmt == "e4m3":
        vals = words.view(ml_dtypes.float8_e4m3fn).astype(np.float64)
    else:
        nib = np.empty((g, 128, n, 4), np.uint8)
        nib[..., 0::2] = words & 0xF
        nib[..., 1::2] = words >> 4
        vals = E2M1[nib]
    vals = vals * np.repeat(np.exp2(scales.astype(np.float64) - 127.0), 8, axis=1)[..., None]
    return vals.transpose(0, 1, 3, 2).reshape(g * 512, n)


D, V, Q, I = 512, 2048, 128, 512


def setup_inputs():
    n = np.random.standard_normal
    idx = np.stack([np.random.permutation(V)[:I] for _ in range(8)])
    fd = mx_kscale(D)
    vocp = pack_weight(n((D, V)) / fd[:, None], "e4m3")
    return {
        "hid": (n((D, Q)) * 1.0 / np.sqrt(D) * fd[:, None]).astype(np.float32),
        "voc_words": vocp[0],
        "voc_scales": vocp[1],
        "mult": (np.random.uniform(100.0, 300.0, (Q, 1))).astype(np.float32),
        "sw": (np.random.uniform(0.005, 0.02, (1, I))).astype(np.float32),
        "dhid": (n((D, Q)) * 1.0 / np.sqrt(D) * fd[:, None]).astype(np.float32),
        "base": (0.5 * n((Q, V))).astype(np.float32),
        "offs": striped8(idx),
    }


def reference(hid, voc_words, voc_scales, mult, sw, dhid, base, offs):
    idx = unstriped8(offs)
    vocu = unpack_weight(voc_words, voc_scales, "e4m3")
    hidq = mxq(f64(hid), 0, "e4m3")
    a = hidq.T @ vocu
    dhidq = mxq(f64(dhid), 0, "e4m3")
    ta = dhidq.T @ vocu
    m1 = np.max(a, axis=1, keepdims=True)
    p = np.exp(a - m1)
    z = np.sum(p, axis=1, keepdims=True)
    px = np.exp(pick8(a, idx, 16) - m1)
    u1 = px / z
    du1 = f64(sw) * (1.0 - u1 * f64(mult)) / u1 + f64(sw) * np.log(u1) * (-1.0) * f64(mult)
    dpx = du1 / z
    dz = np.sum(du1 * px / np.square(z) * (-1.0), axis=1, keepdims=True)
    xp = ta * p
    xz = np.sum(xp, axis=1, keepdims=True)
    xpx = pick8(ta, idx, 16) * px
    xu1 = (xpx - xz * px / z) / z
    xdu1 = (xu1 * f64(mult) * (-1.0) * f64(sw) - xu1 * f64(sw) * (1.0 - u1 * f64(mult)) / u1) / u1 + xu1 / u1 * f64(sw) * (-1.0) * f64(mult)
    xdpx = (xdu1 - xz * du1 / z) / z
    xdz = np.sum((xdu1 * px + xpx * du1 - xz * z * 2.0 * du1 * px / np.square(z)) / np.square(z) * (-1.0), axis=1, keepdims=True)
    xe1 = xdpx * px + xpx * dpx
    xs1 = np.zeros((Q, V))
    xs1[np.arange(Q)[:, None], idx[np.arange(Q) % 128 // 16]] = xe1
    xda = xdz * p + xp * dz + xs1
    y = xda * 64.0 + f64(base)
    return y

@@ -1,0 +1,187 @@
+from contextlib import ExitStack
+import math
+
+import concourse.mybir as mybir
+
+F32 = mybir.dt.float32
+BF16 = mybir.dt.bfloat16
+I32 = mybir.dt.int32
+U32 = mybir.dt.uint32
+U16 = mybir.dt.uint16
+U8 = mybir.dt.uint8
+FP8X4 = mybir.dt.float8_e4m3fn_x4
+ALU = mybir.AluOpType
+ACT = mybir.ActivationFunctionType
+AX = mybir.AxisListType
+
+P = 128
+D, V, Q, I = 512, 2048, 128, 512
+PACK = 4
+N = 512
+CHUNKS = V // N
+GAIN = 64.0
+
+FLOPS = 2 * 2 * D * Q * V
+
+
+def tile_attend_hvfocal_heads_kernel(tc, hid, voc_words, voc_scales, mult, sw, dhid, base, offs, out):
+    nc = tc.nc
+    with ExitStack() as ctx:
+        sb = ctx.enter_context(tc.tile_pool(name="sb", bufs=1))
+        ps = ctx.enter_context(tc.psum_pool(name="ps", bufs=1))
+
+        def col(name):
+            return sb.tile([P, 1], F32, name=name)
+
+        planes = sb.tile([P, N], U8, name="planes", align_bytes=64)
+        nc.vector.memset(planes[:].bitcast(U32), 0)
+        hid_raw = sb.tile([P, PACK, Q], F32, name="hid_raw")
+        nc.sync.dma_start(out=hid_raw[:], in_=hid.rearrange("(p t) q -> p t q", t=PACK))
+        for quad in range(4):
+            nc.sync.dma_start(
+                out=planes[32 * quad : 32 * quad + 16, :].bitcast(I32),
+                in_=voc_scales[0, 4 * quad : 4 * quad + 4, :].bitcast(I32).rearrange("f (c n) -> c f n", c=CHUNKS),
+            )
+        words_hbm = voc_words[0].rearrange("p n t -> p (n t)").bitcast(I32)
+        words = [sb.tile([P, N], U32, name="words%d" % c, align_bytes=64) for c in range(CHUNKS)]
+        nc.sync.dma_start(out=words[0][:].bitcast(I32), in_=words_hbm[:, 0:N])
+        dhid_raw = sb.tile([P, PACK, Q], F32, name="dhid_raw")
+        nc.scalar.dma_start(out=dhid_raw[:], in_=dhid.rearrange("(p t) q -> p t q", t=PACK))
+        for c in range(1, CHUNKS):
+            nc.sync.dma_start(out=words[c][:].bitcast(I32), in_=words_hbm[:, c * N : (c + 1) * N])
+        offsets = sb.tile([P, I // 16], U16, name="offsets")
+        nc.sync.dma_start(offsets[:], offs)
+        sw_all = sb.tile([P, I], F32, name="sw_all")
+        nc.sync.dma_start(out=sw_all[:], in_=sw[0].partition_broadcast(P))
+        mult_sb = col("mult_sb")
+        nc.sync.dma_start(out=mult_sb[:], in_=mult)
+        base_sb = [sb.tile([P, 2 * N], F32, name="base%d" % h) for h in range(2)]
+        for h in range(2):
+            nc.sync.dma_start(out=base_sb[h][:], in_=base[:, h * 2 * N : (h + 1) * 2 * N])
+
+        xs = sb.tile([P, V], F32, name="xs")
+        nc.vector.memset(xs[:], 0.0)
+
+        def quantise(raw, name, weave):
+            woven = sb.tile([P, Q, PACK], BF16, name=name + "_woven", align_bytes=64)
+            weave(
+                out=woven[:].rearrange("p (g i) t -> p g t i", i=4),
+                in_=raw[:].rearrange("p t (g i) -> p g t i", i=4),
+            )
+            codes = sb.tile([P, Q], U32, name=name + "_codes", align_bytes=64)
+            scales = sb.tile([P, Q], U8, name=name + "_scales", align_bytes=64)
+            nc.vector.quantize_mx(codes[:].bitcast(FP8X4), scales[:], woven[:].rearrange("p q t -> p (q t)"))
+            return codes, scales
+
+        def score(operand, c, name, tag):
+            bank = ps.tile([P, N], F32, name=name, tag=tag)
+            nc.tensor.matmul_mx(
+                bank[:],
+                lhsT=operand[0][:].bitcast(FP8X4),
+                lhsT_scale=operand[1][:],
+                rhs=words[c][:].bitcast(FP8X4),
+                rhs_scale=planes[4 * c : P, :],
+                start=True,
+                stop=True,
+            )
+            return bank
+
+        hid_q = quantise(hid_raw, "hid", nc.vector.tensor_copy)
+        dhid_q = quantise(dhid_raw, "dhid", nc.vector.tensor_copy)
+
+        a = sb.tile([P, V], F32, name="a")
+        ta = sb.tile([P, V], F32, name="ta")
+        p = sb.tile([P, V], F32, name="p")
+        xp = sb.tile([P, V], F32, name="xp")
+        part_max = sb.tile([P, CHUNKS], F32, name="part_max")
+        neg_part_max = sb.tile([P, CHUNKS], F32, name="neg_part_max")
+        part_z = sb.tile([P, CHUNKS], F32, name="part_z")
+        part_xz = sb.tile([P, CHUNKS], F32, name="part_xz")
+        chunk = [slice(c * N, (c + 1) * N) for c in range(CHUNKS)]
+        one = [slice(c, c + 1) for c in range(CHUNKS)]
+
+        for c in range(CHUNKS):
+            a_ps = score(hid_q, c, "a_ps%d" % c, "bank%d" % c)
+            nc.vector.tensor_scalar(a[:, chunk[c]], a_ps[:], 1.0, None, ALU.mult, ALU.max, accum_out=part_max[:, one[c]])
+            nc.scalar.activation(neg_part_max[:, one[c]], part_max[:, one[c]], ACT.Identity, scale=-1.0)
+            nc.scalar.activation(
+                p[:, chunk[c]], a[:, chunk[c]], ACT.Exp, bias=neg_part_max[:, one[c]], accum_out=part_z[:, one[c]]
+            )
+        neg_max = col("neg_max")
+        nc.vector.tensor_reduce(neg_max[:], part_max[:], AX.X, ALU.max, negate=True)
+        a_l = sb.tile([P, I], F32, name="a_l")
+        nc.vector.tensor_copy(a_l[:], a[:].indirect(offsets[:]))
+        rescale = sb.tile([P, CHUNKS], F32, name="rescale")
+        nc.scalar.activation(rescale[:], part_max[:], ACT.Exp, bias=neg_max[:])
+        neg_z_parts = sb.tile([P, CHUNKS], F32, name="neg_z_parts")
+        neg_z = col("neg_z")
+        nc.vector.scalar_tensor_tensor(neg_z_parts[:], part_z[:], -1.0, rescale[:], ALU.mult, ALU.mult, accum_out=neg_z[:])
+        neg_rz = col("neg_rz")
+        nc.vector.reciprocal(neg_rz[:], neg_z[:])
+        fac = col("fac")
+        nc.gpsimd.tensor_scalar(fac[:], mult_sb[:], neg_rz[:], 1.0, ALU.mult, ALU.mult)
+
+        ta_ps = []
+        for c in range(CHUNKS):
+            ta_ps.append(score(dhid_q, c, "ta_ps%d" % c, "bank%d" % (CHUNKS + c)))
+            nc.scalar.copy(ta[:, chunk[c]], ta_ps[c][:])
+
+        px = sb.tile([P, I], F32, name="px")
+        nc.scalar.activation(px[:], a_l[:], ACT.Exp, bias=neg_max[:])
+        lnz_less2 = col("lnz_less2")
+        nc.scalar.activation(lnz_less2[:], neg_z[:], ACT.Ln, scale=-math.exp(-2.0))
+        shift = col("shift")
+        nc.scalar.activation(shift[:], lnz_less2[:], ACT.Identity, scale=-1.0, bias=neg_max[:])
+
+        for c in range(CHUNKS):
+            nc.vector.scalar_tensor_tensor(
+                xp[:, chunk[c]], ta_ps[c][:], 1.0, p[:, chunk[c]], ALU.mult, ALU.mult, accum_out=part_xz[:, one[c]]
+            )
+        ta_l = sb.tile([P, I], F32, name="ta_l")
+        nc.vector.tensor_copy(ta_l[:], ta[:].indirect(offsets[:]))
+        mean_parts = sb.tile([P, CHUNKS], F32, name="mean_parts")
+        neg_mean = col("neg_mean")
+        nc.vector.scalar_tensor_tensor(mean_parts[:], part_xz[:], neg_rz[:], rescale[:], ALU.mult, ALU.mult, accum_out=neg_mean[:])
+
+        su = sb.tile([P, I], F32, name="su")
+        su_sum = col("su_sum")
+        nc.vector.scalar_tensor_tensor(su[:], px[:], fac[:], sw_all[:], ALU.mult, ALU.mult, accum_out=su_sum[:])
+        w = sb.tile([P, I], F32, name="w")
+        w_sum = col("w_sum")
+        nc.vector.scalar_tensor_tensor(w[:], a_l[:], shift[:], su[:], ALU.add, ALU.mult, accum_out=w_sum[:])
+        xe = sb.tile([P, I], F32, name="xe")
+        xe_sum = col("xe_sum")
+        nc.vector.scalar_tensor_tensor(xe[:], ta_l[:], neg_mean[:], w[:], ALU.add, ALU.mult, accum_out=xe_sum[:])
+        nc.vector.tensor_copy(xs[:].indirect(offsets[:]), xe[:])
+
+        sw_scaled = sb.tile([P, I], F32, name="sw_scaled")
+        sw_term = col("sw_term")
+        nc.scalar.activation(sw_scaled[:], sw_all[:], ACT.Identity, scale=neg_rz[:], accum_out=sw_term[:])
+        gain = sb.tile([P, CHUNKS], F32, name="gain")
+        nc.scalar.activation(gain[:], rescale[:], ACT.Identity, scale=GAIN)
+        g_part = col("g_part")
+        nc.scalar.activation(g_part[:], su_sum[:], ACT.Identity, scale=-1.0, bias=w_sum[:])
+        dz = col("dz")
+        nc.scalar.activation(dz[:], g_part[:], ACT.Identity, scale=neg_rz[:], bias=sw_term[:])
+        xp_fac = sb.tile([P, CHUNKS], F32, name="xp_fac")
+        nc.scalar.activation(xp_fac[:], gain[:], ACT.Identity, scale=dz[:])
+        mean_term = col("mean_term")
+        nc.scalar.activation(mean_term[:], dz[:], ACT.Identity, scale=neg_mean[:])
+        xdz = col("xdz")
+        nc.scalar.activation(xdz[:], xe_sum[:], ACT.Identity, scale=neg_rz[:], bias=mean_term[:])
+        p_fac = sb.tile([P, CHUNKS], F32, name="p_fac")
+        nc.scalar.activation(p_fac[:], gain[:], ACT.Identity, scale=xdz[:])
+
+        r1 = sb.tile([P, V], F32, name="r1")
+        r2 = sb.tile([P, V], F32, name="r2")
+        for c in range(CHUNKS):
+            half = slice((c % 2) * N, (c % 2 + 1) * N)
+            nc.vector.scalar_tensor_tensor(r1[:, chunk[c]], xp[:, chunk[c]], xp_fac[:, one[c]], base_sb[c // 2][:, half], ALU.mult, ALU.add)
+        for c in range(CHUNKS):
+            nc.vector.scalar_tensor_tensor(r2[:, chunk[c]], p[:, chunk[c]], p_fac[:, one[c]], r1[:, chunk[c]], ALU.mult, ALU.add)
+        edges = [0, 512, 1024, 1536, 1792, 2048]
+        for k in range(len(edges) - 1):
+            cols = slice(edges[k], edges[k + 1])
+            res = sb.tile([P, edges[k + 1] - edges[k]], F32, name="res%d" % k)
+            nc.vector.scalar_tensor_tensor(res[:], xs[:, cols], GAIN, r2[:, cols], ALU.mult, ALU.add)
+            nc.sync.dma_start(out=out[:, cols], in_=res[:])

@@ -1,7 +1,7 @@
 from contextlib import ExitStack
-import math
 
 import concourse.mybir as mybir
+from concourse.masks import make_identity
 
 F32 = mybir.dt.float32
 BF16 = mybir.dt.bfloat16
@@ -20,6 +20,7 @@ PACK = 4
 N = 512
 CHUNKS = V // N
 GAIN = 64.0
+BLOCKS = N // P
 
 FLOPS = 2 * 2 * D * Q * V
 
@@ -59,6 +60,8 @@ def tile_attend_hvfocal_heads_kernel(tc, hid, voc_words, voc_scales, mult, sw, d
         for h in range(2):
             nc.sync.dma_start(out=base_sb[h][:], in_=base[:, h * 2 * N : (h + 1) * 2 * N])
 
+        ident = sb.tile([P, P], F32, name="ident")
+        make_identity(nc, ident[:])
         xs = sb.tile([P, V], F32, name="xs")
         nc.vector.memset(xs[:], 0.0)
 
@@ -93,59 +96,64 @@ def tile_attend_hvfocal_heads_kernel(tc, hid, voc_words, voc_scales, mult, sw, d
         ta = sb.tile([P, V], F32, name="ta")
         p = sb.tile([P, V], F32, name="p")
         xp = sb.tile([P, V], F32, name="xp")
-        part_max = sb.tile([P, CHUNKS], F32, name="part_max")
-        neg_part_max = sb.tile([P, CHUNKS], F32, name="neg_part_max")
-        part_z = sb.tile([P, CHUNKS], F32, name="part_z")
-        part_xz = sb.tile([P, CHUNKS], F32, name="part_xz")
+        a_l = sb.tile([P, I], F32, name="a_l")
+        part_max = a_l[:, 0:CHUNKS]
         chunk = [slice(c * N, (c + 1) * N) for c in range(CHUNKS)]
-        one = [slice(c, c + 1) for c in range(CHUNKS)]
+        first, rest = chunk[0], slice(N, V)
 
         for c in range(CHUNKS):
             a_ps = score(hid_q, c, "a_ps%d" % c, "bank%d" % c)
-            nc.vector.tensor_scalar(a[:, chunk[c]], a_ps[:], 1.0, None, ALU.mult, ALU.max, accum_out=part_max[:, one[c]])
-            nc.scalar.activation(neg_part_max[:, one[c]], part_max[:, one[c]], ACT.Identity, scale=-1.0)
-            nc.scalar.activation(
-                p[:, chunk[c]], a[:, chunk[c]], ACT.Exp, bias=neg_part_max[:, one[c]], accum_out=part_z[:, one[c]]
-            )
-        neg_max = col("neg_max")
-        nc.vector.tensor_reduce(neg_max[:], part_max[:], AX.X, ALU.max, negate=True)
-        a_l = sb.tile([P, I], F32, name="a_l")
-        nc.vector.tensor_copy(a_l[:], a[:].indirect(offsets[:]))
-        rescale = sb.tile([P, CHUNKS], F32, name="rescale")
-        nc.scalar.activation(rescale[:], part_max[:], ACT.Exp, bias=neg_max[:])
-        neg_z_parts = sb.tile([P, CHUNKS], F32, name="neg_z_parts")
-        neg_z = col("neg_z")
-        nc.vector.scalar_tensor_tensor(neg_z_parts[:], part_z[:], -1.0, rescale[:], ALU.mult, ALU.mult, accum_out=neg_z[:])
-        neg_rz = col("neg_rz")
-        nc.vector.reciprocal(neg_rz[:], neg_z[:])
-        fac = col("fac")
-        nc.gpsimd.tensor_scalar(fac[:], mult_sb[:], neg_rz[:], 1.0, ALU.mult, ALU.mult)
-
-        ta_ps = []
+            nc.vector.tensor_scalar(a[:, chunk[c]], a_ps[:], 1.0, None, ALU.mult, ALU.max, accum_out=part_max[:, c : c + 1])
+        neg_first_max = col("neg_first_max")
+        nc.scalar.activation(neg_first_max[:], part_max[:, 0:1], ACT.Identity, scale=-1.0)
+        z_first = col("z_first")
+        nc.scalar.activation(p[:, first], a[:, first], ACT.Exp, bias=neg_first_max[:], accum_out=z_first[:])
         for c in range(CHUNKS):
-            ta_ps.append(score(dhid_q, c, "ta_ps%d" % c, "bank%d" % (CHUNKS + c)))
-            nc.scalar.copy(ta[:, chunk[c]], ta_ps[c][:])
+            ta_ps = score(dhid_q, c, "ta_ps%d" % c, "bank%d" % (CHUNKS + c))
+            nc.scalar.copy(ta[:, chunk[c]], ta_ps[:])
 
+        neg_max = col("neg_max")
+        nc.vector.tensor_reduce(neg_max[:], part_max, AX.X, ALU.max, negate=True)
+        nc.vector.tensor_copy(a_l[:], a[:].indirect(offsets[:]))
+        rescale = col("rescale")
+        nc.scalar.activation(rescale[:], neg_first_max[:], ACT.Exp, scale=-1.0, bias=neg_max[:])
+        z_rest = col("z_rest")
+        nc.scalar.activation(p[:, rest], a[:, rest], ACT.Exp, bias=neg_max[:], accum_out=z_rest[:])
+        z_head = col("z_head")
+        nc.scalar.activation(z_head[:], z_first[:], ACT.Identity, scale=rescale[:])
         px = sb.tile([P, I], F32, name="px")
         nc.scalar.activation(px[:], a_l[:], ACT.Exp, bias=neg_max[:])
-        lnz_less2 = col("lnz_less2")
-        nc.scalar.activation(lnz_less2[:], neg_z[:], ACT.Ln, scale=-math.exp(-2.0))
+        sw_scaled = sb.tile([P, I], F32, name="sw_scaled")
+        ln_z = sw_scaled[:, 0:1]
+        nc.scalar.activation(ln_z, z_rest[:], ACT.Ln, bias=z_head[:])
+        two_less_max = col("two_less_max")
+        nc.vector.tensor_scalar(two_less_max[:], neg_max[:], 2.0, None, ALU.add)
         shift = col("shift")
-        nc.scalar.activation(shift[:], lnz_less2[:], ACT.Identity, scale=-1.0, bias=neg_max[:])
+        nc.scalar.activation(shift[:], ln_z, ACT.Identity, scale=-1.0, bias=two_less_max[:])
 
-        for c in range(CHUNKS):
-            nc.vector.scalar_tensor_tensor(
-                xp[:, chunk[c]], ta_ps[c][:], 1.0, p[:, chunk[c]], ALU.mult, ALU.mult, accum_out=part_xz[:, one[c]]
-            )
+        neg_z = col("neg_z")
+        nc.vector.tensor_scalar(neg_z[:], z_rest[:], z_head[:], -1.0, ALU.add, ALU.mult)
+        neg_rz = col("neg_rz")
+        nc.vector.reciprocal(neg_rz[:], neg_z[:])
+        xz_first = col("xz_first")
+        nc.vector.scalar_tensor_tensor(
+            xp[:, first], ta[:, first], rescale[:], p[:, first], ALU.mult, ALU.mult, accum_out=xz_first[:]
+        )
         ta_l = sb.tile([P, I], F32, name="ta_l")
         nc.vector.tensor_copy(ta_l[:], ta[:].indirect(offsets[:]))
-        mean_parts = sb.tile([P, CHUNKS], F32, name="mean_parts")
+        xz_rest = col("xz_rest")
+        nc.vector.scalar_tensor_tensor(xp[:, rest], ta[:, rest], 1.0, p[:, rest], ALU.mult, ALU.mult, accum_out=xz_rest[:])
         neg_mean = col("neg_mean")
-        nc.vector.scalar_tensor_tensor(mean_parts[:], part_xz[:], neg_rz[:], rescale[:], ALU.mult, ALU.mult, accum_out=neg_mean[:])
+        nc.vector.tensor_scalar(neg_mean[:], xz_rest[:], xz_first[:], neg_rz[:], ALU.add, ALU.mult)
+        gains = sb.tile([P, 2], F32, name="gains")
+        nc.vector.memset(gains[:, 0:1], -GAIN)
+        nc.vector.memset(gains[:, 1:2], GAIN)
+        gain_zz = sb.tile([P, 2], F32, name="gain_zz")
+        nc.vector.tensor_scalar(gain_zz[:], gains[:], neg_rz[:], neg_rz[:], ALU.mult, ALU.mult)
 
         su = sb.tile([P, I], F32, name="su")
         su_sum = col("su_sum")
-        nc.vector.scalar_tensor_tensor(su[:], px[:], fac[:], sw_all[:], ALU.mult, ALU.mult, accum_out=su_sum[:])
+        nc.vector.scalar_tensor_tensor(su[:], px[:], mult_sb[:], sw_all[:], ALU.mult, ALU.mult, accum_out=su_sum[:])
         w = sb.tile([P, I], F32, name="w")
         w_sum = col("w_sum")
         nc.vector.scalar_tensor_tensor(w[:], a_l[:], shift[:], su[:], ALU.add, ALU.mult, accum_out=w_sum[:])
@@ -154,34 +162,67 @@ def tile_attend_hvfocal_heads_kernel(tc, hid, voc_words, voc_scales, mult, sw, d
         nc.vector.scalar_tensor_tensor(xe[:], ta_l[:], neg_mean[:], w[:], ALU.add, ALU.mult, accum_out=xe_sum[:])
         nc.vector.tensor_copy(xs[:].indirect(offsets[:]), xe[:])
 
-        sw_scaled = sb.tile([P, I], F32, name="sw_scaled")
+        gain_z = col("gain_z")
+        nc.scalar.activation(gain_z[:], neg_rz[:], ACT.Identity, scale=GAIN)
         sw_term = col("sw_term")
-        nc.scalar.activation(sw_scaled[:], sw_all[:], ACT.Identity, scale=neg_rz[:], accum_out=sw_term[:])
-        gain = sb.tile([P, CHUNKS], F32, name="gain")
-        nc.scalar.activation(gain[:], rescale[:], ACT.Identity, scale=GAIN)
-        g_part = col("g_part")
-        nc.scalar.activation(g_part[:], su_sum[:], ACT.Identity, scale=-1.0, bias=w_sum[:])
-        dz = col("dz")
-        nc.scalar.activation(dz[:], g_part[:], ACT.Identity, scale=neg_rz[:], bias=sw_term[:])
-        xp_fac = sb.tile([P, CHUNKS], F32, name="xp_fac")
-        nc.scalar.activation(xp_fac[:], gain[:], ACT.Identity, scale=dz[:])
+        nc.scalar.activation(sw_scaled[:], sw_all[:], ACT.Identity, scale=gain_z[:], accum_out=sw_term[:])
+        dz_part = col("dz_part")
+        nc.scalar.activation(dz_part[:], su_sum[:], ACT.Identity, scale=gain_zz[:, 0:1], bias=sw_term[:])
+        xp_fac = col("xp_fac")
+        nc.scalar.activation(xp_fac[:], w_sum[:], ACT.Identity, scale=gain_zz[:, 1:2], bias=dz_part[:])
         mean_term = col("mean_term")
-        nc.scalar.activation(mean_term[:], dz[:], ACT.Identity, scale=neg_mean[:])
-        xdz = col("xdz")
-        nc.scalar.activation(xdz[:], xe_sum[:], ACT.Identity, scale=neg_rz[:], bias=mean_term[:])
-        p_fac = sb.tile([P, CHUNKS], F32, name="p_fac")
-        nc.scalar.activation(p_fac[:], gain[:], ACT.Identity, scale=xdz[:])
+        nc.scalar.activation(mean_term[:], xp_fac[:], ACT.Identity, scale=neg_mean[:])
+        p_fac = col("p_fac")
+        nc.scalar.activation(p_fac[:], xe_sum[:], ACT.Identity, scale=gain_zz[:, 1:2], bias=mean_term[:])
+        p_fac_first = col("p_fac_first")
+        nc.scalar.activation(p_fac_first[:], p_fac[:], ACT.Identity, scale=rescale[:])
 
-        r1 = sb.tile([P, V], F32, name="r1")
-        r2 = sb.tile([P, V], F32, name="r2")
-        for c in range(CHUNKS):
-            half = slice((c % 2) * N, (c % 2 + 1) * N)
-            nc.vector.scalar_tensor_tensor(r1[:, chunk[c]], xp[:, chunk[c]], xp_fac[:, one[c]], base_sb[c // 2][:, half], ALU.mult, ALU.add)
-        for c in range(CHUNKS):
-            nc.vector.scalar_tensor_tensor(r2[:, chunk[c]], p[:, chunk[c]], p_fac[:, one[c]], r1[:, chunk[c]], ALU.mult, ALU.add)
-        edges = [0, 512, 1024, 1536, 1792, 2048]
-        for k in range(len(edges) - 1):
-            cols = slice(edges[k], edges[k + 1])
-            res = sb.tile([P, edges[k + 1] - edges[k]], F32, name="res%d" % k)
-            nc.vector.scalar_tensor_tensor(res[:], xs[:, cols], GAIN, r2[:, cols], ALU.mult, ALU.add)
-            nc.sync.dma_start(out=out[:, cols], in_=res[:])
+        def base_cols(c):
+            return base_sb[c // 2][:, (c % 2) * N : (c % 2 + 1) * N]
+
+        def finish(c, dense, pieces):
+            width = N // pieces
+            for k in range(pieces):
+                inside = slice(k * width, (k + 1) * width)
+                cols = slice(c * N + k * width, c * N + (k + 1) * width)
+                res = sb.tile([P, width], F32, name="res%d_%d" % (c, k))
+                nc.vector.scalar_tensor_tensor(res[:], xs[:, cols], gain_z[:], dense[:, inside], ALU.mult, ALU.add)
+                nc.sync.dma_start(out=out[:, cols], in_=res[:])
+
+        def turn(bank, term, start, stop):
+            for b in range(BLOCKS):
+                blk = slice(b * P, (b + 1) * P)
+                nc.tensor.matmul(
+                    bank[:, blk],
+                    lhsT=term[:, blk],
+                    rhs=ident[:],
+                    is_transpose=True,
+                    start=start and b == 0,
+                    stop=stop and b == BLOCKS - 1,
+                )
+
+        r1 = sb.tile([P, N], F32, name="r1")
+        nc.vector.scalar_tensor_tensor(r1[:], xp[:, first], xp_fac[:], base_cols(0), ALU.mult, ALU.add)
+        r2 = sb.tile([P, N], F32, name="r2")
+        nc.vector.scalar_tensor_tensor(r2[:], p[:, first], p_fac_first[:], r1[:], ALU.mult, ALU.add)
+        finish(0, r2, 1)
+
+        turned = range(1, CHUNKS)
+        sum_ps = {c: ps.tile([P, N], F32, name="sum_ps%d" % c, tag="bank%d" % c) for c in turned}
+        for c in turned:
+            turn(sum_ps[c], base_cols(c), True, False)
+        for c in turned:
+            xp_term = sb.tile([P, N], F32, name="xp_term%d" % c)
+            nc.scalar.activation(xp_term[:], xp[:, chunk[c]], ACT.Identity, scale=xp_fac[:])
+            turn(sum_ps[c], xp_term, False, False)
+            p_term = sb.tile([P, N], F32, name="p_term%d" % c)
+            nc.scalar.activation(p_term[:], p[:, chunk[c]], ACT.Identity, scale=p_fac[:])
+            turn(sum_ps[c], p_term, False, True)
+        for c in turned:
+            sum_sb = sb.tile([P, N], F32, name="sum_sb%d" % c)
+            nc.scalar.copy(sum_sb[:], sum_ps[c][:])
+            dense_ps = ps.tile([P, N], F32, name="dense_ps%d" % c, tag="bank%d" % (CHUNKS + c))
+            for b in range(BLOCKS):
+                blk = slice(b * P, (b + 1) * P)
+                nc.tensor.transpose(dense_ps[:, blk], sum_sb[:, blk], ident[:])
+            finish(c, dense_ps, 2 if c == CHUNKS - 1 else 1)

@@ -139,8 +139,6 @@ def tile_attend_hvfocal_heads_kernel(tc, hid, voc_words, voc_scales, mult, sw, d
         nc.vector.scalar_tensor_tensor(
             xp[:, first], ta[:, first], rescale[:], p[:, first], ALU.mult, ALU.mult, accum_out=xz_first[:]
         )
-        ta_l = sb.tile([P, I], F32, name="ta_l")
-        nc.vector.tensor_copy(ta_l[:], ta[:].indirect(offsets[:]))
         xz_rest = col("xz_rest")
         nc.vector.scalar_tensor_tensor(xp[:, rest], ta[:, rest], 1.0, p[:, rest], ALU.mult, ALU.mult, accum_out=xz_rest[:])
         neg_mean = col("neg_mean")
@@ -157,6 +155,8 @@ def tile_attend_hvfocal_heads_kernel(tc, hid, voc_words, voc_scales, mult, sw, d
         w = sb.tile([P, I], F32, name="w")
         w_sum = col("w_sum")
         nc.vector.scalar_tensor_tensor(w[:], a_l[:], shift[:], su[:], ALU.add, ALU.mult, accum_out=w_sum[:])
+        ta_l = su
+        nc.vector.tensor_copy(ta_l[:], ta[:].indirect(offsets[:]))
         xe = sb.tile([P, I], F32, name="xe")
         xe_sum = col("xe_sum")
         nc.vector.scalar_tensor_tensor(xe[:], ta_l[:], neg_mean[:], w[:], ALU.add, ALU.mult, accum_out=xe_sum[:])
@@ -172,10 +172,6 @@ def tile_attend_hvfocal_heads_kernel(tc, hid, voc_words, voc_scales, mult, sw, d
         nc.scalar.activation(xp_fac[:], w_sum[:], ACT.Identity, scale=gain_zz[:, 1:2], bias=dz_part[:])
         mean_term = col("mean_term")
         nc.scalar.activation(mean_term[:], xp_fac[:], ACT.Identity, scale=neg_mean[:])
-        p_fac = col("p_fac")
-        nc.scalar.activation(p_fac[:], xe_sum[:], ACT.Identity, scale=gain_zz[:, 1:2], bias=mean_term[:])
-        p_fac_first = col("p_fac_first")
-        nc.scalar.activation(p_fac_first[:], p_fac[:], ACT.Identity, scale=rescale[:])
 
         def base_cols(c):
             return base_sb[c // 2][:, (c % 2) * N : (c % 2 + 1) * N]
@@ -201,12 +197,6 @@ def tile_attend_hvfocal_heads_kernel(tc, hid, voc_words, voc_scales, mult, sw, d
                     stop=stop and b == BLOCKS - 1,
                 )
 
-        r1 = sb.tile([P, N], F32, name="r1")
-        nc.vector.scalar_tensor_tensor(r1[:], xp[:, first], xp_fac[:], base_cols(0), ALU.mult, ALU.add)
-        r2 = sb.tile([P, N], F32, name="r2")
-        nc.vector.scalar_tensor_tensor(r2[:], p[:, first], p_fac_first[:], r1[:], ALU.mult, ALU.add)
-        finish(0, r2, 1)
-
         turned = range(1, CHUNKS)
         sum_ps = {c: ps.tile([P, N], F32, name="sum_ps%d" % c, tag="bank%d" % c) for c in turned}
         for c in turned:
@@ -215,6 +205,18 @@ def tile_attend_hvfocal_heads_kernel(tc, hid, voc_words, voc_scales, mult, sw, d
             xp_term = sb.tile([P, N], F32, name="xp_term%d" % c)
             nc.scalar.activation(xp_term[:], xp[:, chunk[c]], ACT.Identity, scale=xp_fac[:])
             turn(sum_ps[c], xp_term, False, False)
+        p_fac = col("p_fac")
+        nc.scalar.activation(p_fac[:], xe_sum[:], ACT.Identity, scale=gain_zz[:, 1:2], bias=mean_term[:])
+        p_fac_first = col("p_fac_first")
+        nc.scalar.activation(p_fac_first[:], p_fac[:], ACT.Identity, scale=rescale[:])
+
+        r1 = sb.tile([P, N], F32, name="r1")
+        nc.vector.scalar_tensor_tensor(r1[:], xp[:, first], xp_fac[:], base_cols(0), ALU.mult, ALU.add)
+        r2 = sb.tile([P, N], F32, name="r2")
+        nc.vector.scalar_tensor_tensor(r2[:], p[:, first], p_fac_first[:], r1[:], ALU.mult, ALU.add)
+        finish(0, r2, 1)
+
+        for c in turned:
             p_term = sb.tile([P, N], F32, name="p_term%d" % c)
             nc.scalar.activation(p_term[:], p[:, chunk[c]], ACT.Identity, scale=p_fac[:])
             turn(sum_ps[c], p_term, False, True)

@@ -19,8 +19,10 @@ D, V, Q, I = 512, 2048, 128, 512
 PACK = 4
 N = 512
 CHUNKS = V // N
+QUADRANTS = 4
 GAIN = 64.0
 BLOCKS = N // P
+LAST_PIECES = 2
 
 FLOPS = 2 * 2 * D * Q * V
 
@@ -38,7 +40,7 @@ def tile_attend_hvfocal_heads_kernel(tc, hid, voc_words, voc_scales, mult, sw, d
         nc.vector.memset(planes[:].bitcast(U32), 0)
         hid_raw = sb.tile([P, PACK, Q], F32, name="hid_raw")
         nc.sync.dma_start(out=hid_raw[:], in_=hid.rearrange("(p t) q -> p t q", t=PACK))
-        for quad in range(4):
+        for quad in range(QUADRANTS):
             nc.sync.dma_start(
                 out=planes[32 * quad : 32 * quad + 16, :].bitcast(I32),
                 in_=voc_scales[0, 4 * quad : 4 * quad + 4, :].bitcast(I32).rearrange("f (c n) -> c f n", c=CHUNKS),
@@ -65,9 +67,9 @@ def tile_attend_hvfocal_heads_kernel(tc, hid, voc_words, voc_scales, mult, sw, d
         xs = sb.tile([P, V], F32, name="xs")
         nc.vector.memset(xs[:], 0.0)
 
-        def quantise(raw, name, weave):
+        def quantise(raw, name):
             woven = sb.tile([P, Q, PACK], BF16, name=name + "_woven", align_bytes=64)
-            weave(
+            nc.vector.tensor_copy(
                 out=woven[:].rearrange("p (g i) t -> p g t i", i=4),
                 in_=raw[:].rearrange("p t (g i) -> p g t i", i=4),
             )
@@ -89,8 +91,8 @@ def tile_attend_hvfocal_heads_kernel(tc, hid, voc_words, voc_scales, mult, sw, d
             )
             return bank
 
-        hid_q = quantise(hid_raw, "hid", nc.vector.tensor_copy)
-        dhid_q = quantise(dhid_raw, "dhid", nc.vector.tensor_copy)
+        hid_q = quantise(hid_raw, "hid")
+        dhid_q = quantise(dhid_raw, "dhid")
 
         a = sb.tile([P, V], F32, name="a")
         ta = sb.tile([P, V], F32, name="ta")
@@ -103,7 +105,9 @@ def tile_attend_hvfocal_heads_kernel(tc, hid, voc_words, voc_scales, mult, sw, d
 
         for c in range(CHUNKS):
             a_ps = score(hid_q, c, "a_ps%d" % c, "bank%d" % c)
-            nc.vector.tensor_scalar(a[:, chunk[c]], a_ps[:], 1.0, None, ALU.mult, ALU.max, accum_out=part_max[:, c : c + 1])
+            nc.vector.tensor_scalar(
+                a[:, chunk[c]], a_ps[:], 1.0, None, ALU.mult, ALU.max, accum_out=part_max[:, c : c + 1]
+            )
         neg_first_max = col("neg_first_max")
         nc.scalar.activation(neg_first_max[:], part_max[:, 0:1], ACT.Identity, scale=-1.0)
         z_first = col("z_first")
@@ -115,6 +119,7 @@ def tile_attend_hvfocal_heads_kernel(tc, hid, voc_words, voc_scales, mult, sw, d
         neg_max = col("neg_max")
         nc.vector.tensor_reduce(neg_max[:], part_max, AX.X, ALU.max, negate=True)
         nc.vector.tensor_copy(a_l[:], a[:].indirect(offsets[:]))
+
         rescale = col("rescale")
         nc.scalar.activation(rescale[:], neg_first_max[:], ACT.Exp, scale=-1.0, bias=neg_max[:])
         z_rest = col("z_rest")
@@ -140,7 +145,9 @@ def tile_attend_hvfocal_heads_kernel(tc, hid, voc_words, voc_scales, mult, sw, d
             xp[:, first], ta[:, first], rescale[:], p[:, first], ALU.mult, ALU.mult, accum_out=xz_first[:]
         )
         xz_rest = col("xz_rest")
-        nc.vector.scalar_tensor_tensor(xp[:, rest], ta[:, rest], 1.0, p[:, rest], ALU.mult, ALU.mult, accum_out=xz_rest[:])
+        nc.vector.scalar_tensor_tensor(
+            xp[:, rest], ta[:, rest], 1.0, p[:, rest], ALU.mult, ALU.mult, accum_out=xz_rest[:]
+        )
         neg_mean = col("neg_mean")
         nc.vector.tensor_scalar(neg_mean[:], xz_rest[:], xz_first[:], neg_rz[:], ALU.add, ALU.mult)
         gains = sb.tile([P, 2], F32, name="gains")
@@ -197,6 +204,13 @@ def tile_attend_hvfocal_heads_kernel(tc, hid, voc_words, voc_scales, mult, sw, d
                     stop=stop and b == BLOCKS - 1,
                 )
 
+        ta_fac_first = col("ta_fac_first")
+        nc.scalar.activation(ta_fac_first[:], xp_fac[:], ACT.Identity, scale=rescale[:])
+        mean_term_first = col("mean_term_first")
+        nc.scalar.activation(mean_term_first[:], mean_term[:], ACT.Identity, scale=rescale[:])
+        gain_zz_first = col("gain_zz_first")
+        nc.scalar.activation(gain_zz_first[:], gain_zz[:, 1:2], ACT.Identity, scale=rescale[:])
+
         turned = range(1, CHUNKS)
         sum_ps = {c: ps.tile([P, N], F32, name="sum_ps%d" % c, tag="bank%d" % c) for c in turned}
         for c in turned:
@@ -205,16 +219,18 @@ def tile_attend_hvfocal_heads_kernel(tc, hid, voc_words, voc_scales, mult, sw, d
             xp_term = sb.tile([P, N], F32, name="xp_term%d" % c)
             nc.scalar.activation(xp_term[:], xp[:, chunk[c]], ACT.Identity, scale=xp_fac[:])
             turn(sum_ps[c], xp_term, False, False)
+        p_fac_first = col("p_fac_first")
+        nc.scalar.activation(p_fac_first[:], xe_sum[:], ACT.Identity, scale=gain_zz_first[:], bias=mean_term_first[:])
         p_fac = col("p_fac")
         nc.scalar.activation(p_fac[:], xe_sum[:], ACT.Identity, scale=gain_zz[:, 1:2], bias=mean_term[:])
-        p_fac_first = col("p_fac_first")
-        nc.scalar.activation(p_fac_first[:], p_fac[:], ACT.Identity, scale=rescale[:])
 
-        r1 = sb.tile([P, N], F32, name="r1")
-        nc.vector.scalar_tensor_tensor(r1[:], xp[:, first], xp_fac[:], base_cols(0), ALU.mult, ALU.add)
-        r2 = sb.tile([P, N], F32, name="r2")
-        nc.vector.scalar_tensor_tensor(r2[:], p[:, first], p_fac_first[:], r1[:], ALU.mult, ALU.add)
-        finish(0, r2, 1)
+        slope = sb.tile([P, N], F32, name="slope")
+        nc.gpsimd.tensor_scalar(slope[:], ta[:, first], ta_fac_first[:], p_fac_first[:], ALU.mult, ALU.add)
+        spread = sb.tile([P, N], F32, name="spread")
+        nc.gpsimd.tensor_tensor(spread[:], slope[:], p[:, first], ALU.mult)
+        dense_first = sb.tile([P, N], F32, name="dense_first")
+        nc.vector.tensor_tensor(dense_first[:], spread[:], base_cols(0), ALU.add)
+        finish(0, dense_first, 1)
 
         for c in turned:
             p_term = sb.tile([P, N], F32, name="p_term%d" % c)
@@ -227,4 +243,4 @@ def tile_attend_hvfocal_heads_kernel(tc, hid, voc_words, voc_scales, mult, sw, d
             for b in range(BLOCKS):
                 blk = slice(b * P, (b + 1) * P)
                 nc.tensor.transpose(dense_ps[:, blk], sum_sb[:, blk], ident[:])
-            finish(c, dense_ps, 2 if c == CHUNKS - 1 else 1)
+            finish(c, dense_ps, LAST_PIECES if c == CHUNKS - 1 else 1)

from contextlib import ExitStack

import concourse.mybir as mybir
from concourse.masks import make_identity

F32 = mybir.dt.float32
BF16 = mybir.dt.bfloat16
I32 = mybir.dt.int32
U32 = mybir.dt.uint32
U16 = mybir.dt.uint16
U8 = mybir.dt.uint8
FP8X4 = mybir.dt.float8_e4m3fn_x4
ALU = mybir.AluOpType
ACT = mybir.ActivationFunctionType
AX = mybir.AxisListType

P = 128
D, V, Q, I = 512, 2048, 128, 512
PACK = 4
N = 512
CHUNKS = V // N
QUADRANTS = 4
GAIN = 64.0
BLOCKS = N // P
LAST_PIECES = 2

FLOPS = 2 * 2 * D * Q * V


def tile_attend_hvfocal_heads_kernel(tc, hid, voc_words, voc_scales, mult, sw, dhid, base, offs, out):
    nc = tc.nc
    with ExitStack() as ctx:
        sb = ctx.enter_context(tc.tile_pool(name="sb", bufs=1))
        ps = ctx.enter_context(tc.psum_pool(name="ps", bufs=1))

        def col(name):
            return sb.tile([P, 1], F32, name=name)

        planes = sb.tile([P, N], U8, name="planes", align_bytes=64)
        nc.vector.memset(planes[:].bitcast(U32), 0)
        hid_raw = sb.tile([P, PACK, Q], F32, name="hid_raw")
        nc.sync.dma_start(out=hid_raw[:], in_=hid.rearrange("(p t) q -> p t q", t=PACK))
        for quad in range(QUADRANTS):
            nc.sync.dma_start(
                out=planes[32 * quad : 32 * quad + 16, :].bitcast(I32),
                in_=voc_scales[0, 4 * quad : 4 * quad + 4, :].bitcast(I32).rearrange("f (c n) -> c f n", c=CHUNKS),
            )
        words_hbm = voc_words[0].rearrange("p n t -> p (n t)").bitcast(I32)
        words = [sb.tile([P, N], U32, name="words%d" % c, align_bytes=64) for c in range(CHUNKS)]
        nc.sync.dma_start(out=words[0][:].bitcast(I32), in_=words_hbm[:, 0:N])
        dhid_raw = sb.tile([P, PACK, Q], F32, name="dhid_raw")
        nc.scalar.dma_start(out=dhid_raw[:], in_=dhid.rearrange("(p t) q -> p t q", t=PACK))
        for c in range(1, CHUNKS):
            nc.sync.dma_start(out=words[c][:].bitcast(I32), in_=words_hbm[:, c * N : (c + 1) * N])
        offsets = sb.tile([P, I // 16], U16, name="offsets")
        nc.sync.dma_start(offsets[:], offs)
        sw_all = sb.tile([P, I], F32, name="sw_all")
        nc.sync.dma_start(out=sw_all[:], in_=sw[0].partition_broadcast(P))
        mult_sb = col("mult_sb")
        nc.sync.dma_start(out=mult_sb[:], in_=mult)
        base_sb = [sb.tile([P, 2 * N], F32, name="base%d" % h) for h in range(2)]
        for h in range(2):
            nc.sync.dma_start(out=base_sb[h][:], in_=base[:, h * 2 * N : (h + 1) * 2 * N])

        ident = sb.tile([P, P], F32, name="ident")
        make_identity(nc, ident[:])
        xs = sb.tile([P, V], F32, name="xs")
        nc.vector.memset(xs[:], 0.0)

        def quantise(raw, name):
            woven = sb.tile([P, Q, PACK], BF16, name=name + "_woven", align_bytes=64)
            nc.vector.tensor_copy(
                out=woven[:].rearrange("p (g i) t -> p g t i", i=4),
                in_=raw[:].rearrange("p t (g i) -> p g t i", i=4),
            )
            codes = sb.tile([P, Q], U32, name=name + "_codes", align_bytes=64)
            scales = sb.tile([P, Q], U8, name=name + "_scales", align_bytes=64)
            nc.vector.quantize_mx(codes[:].bitcast(FP8X4), scales[:], woven[:].rearrange("p q t -> p (q t)"))
            return codes, scales

        def score(operand, c, name, tag):
            bank = ps.tile([P, N], F32, name=name, tag=tag)
            nc.tensor.matmul_mx(
                bank[:],
                lhsT=operand[0][:].bitcast(FP8X4),
                lhsT_scale=operand[1][:],
                rhs=words[c][:].bitcast(FP8X4),
                rhs_scale=planes[4 * c : P, :],
                start=True,
                stop=True,
            )
            return bank

        hid_q = quantise(hid_raw, "hid")
        dhid_q = quantise(dhid_raw, "dhid")

        a = sb.tile([P, V], F32, name="a")
        ta = sb.tile([P, V], F32, name="ta")
        p = sb.tile([P, V], F32, name="p")
        xp = sb.tile([P, V], F32, name="xp")
        a_l = sb.tile([P, I], F32, name="a_l")
        part_max = a_l[:, 0:CHUNKS]
        chunk = [slice(c * N, (c + 1) * N) for c in range(CHUNKS)]
        first, rest = chunk[0], slice(N, V)

        for c in range(CHUNKS):
            a_ps = score(hid_q, c, "a_ps%d" % c, "bank%d" % c)
            nc.vector.tensor_scalar(
                a[:, chunk[c]], a_ps[:], 1.0, None, ALU.mult, ALU.max, accum_out=part_max[:, c : c + 1]
            )
        neg_first_max = col("neg_first_max")
        nc.scalar.activation(neg_first_max[:], part_max[:, 0:1], ACT.Identity, scale=-1.0)
        z_first = col("z_first")
        nc.scalar.activation(p[:, first], a[:, first], ACT.Exp, bias=neg_first_max[:], accum_out=z_first[:])
        for c in range(CHUNKS):
            ta_ps = score(dhid_q, c, "ta_ps%d" % c, "bank%d" % (CHUNKS + c))
            nc.scalar.copy(ta[:, chunk[c]], ta_ps[:])

        neg_max = col("neg_max")
        nc.vector.tensor_reduce(neg_max[:], part_max, AX.X, ALU.max, negate=True)
        nc.vector.tensor_copy(a_l[:], a[:].indirect(offsets[:]))

        rescale = col("rescale")
        nc.scalar.activation(rescale[:], neg_first_max[:], ACT.Exp, scale=-1.0, bias=neg_max[:])
        z_rest = col("z_rest")
        nc.scalar.activation(p[:, rest], a[:, rest], ACT.Exp, bias=neg_max[:], accum_out=z_rest[:])
        z_head = col("z_head")
        nc.scalar.activation(z_head[:], z_first[:], ACT.Identity, scale=rescale[:])
        px = sb.tile([P, I], F32, name="px")
        nc.scalar.activation(px[:], a_l[:], ACT.Exp, bias=neg_max[:])
        sw_scaled = sb.tile([P, I], F32, name="sw_scaled")
        ln_z = sw_scaled[:, 0:1]
        nc.scalar.activation(ln_z, z_rest[:], ACT.Ln, bias=z_head[:])
        two_less_max = col("two_less_max")
        nc.vector.tensor_scalar(two_less_max[:], neg_max[:], 2.0, None, ALU.add)
        shift = col("shift")
        nc.scalar.activation(shift[:], ln_z, ACT.Identity, scale=-1.0, bias=two_less_max[:])

        neg_z = col("neg_z")
        nc.vector.tensor_scalar(neg_z[:], z_rest[:], z_head[:], -1.0, ALU.add, ALU.mult)
        neg_rz = col("neg_rz")
        nc.vector.reciprocal(neg_rz[:], neg_z[:])
        xz_first = col("xz_first")
        nc.vector.scalar_tensor_tensor(
            xp[:, first], ta[:, first], rescale[:], p[:, first], ALU.mult, ALU.mult, accum_out=xz_first[:]
        )
        xz_rest = col("xz_rest")
        nc.vector.scalar_tensor_tensor(
            xp[:, rest], ta[:, rest], 1.0, p[:, rest], ALU.mult, ALU.mult, accum_out=xz_rest[:]
        )
        neg_mean = col("neg_mean")
        nc.vector.tensor_scalar(neg_mean[:], xz_rest[:], xz_first[:], neg_rz[:], ALU.add, ALU.mult)
        gains = sb.tile([P, 2], F32, name="gains")
        nc.vector.memset(gains[:, 0:1], -GAIN)
        nc.vector.memset(gains[:, 1:2], GAIN)
        gain_zz = sb.tile([P, 2], F32, name="gain_zz")
        nc.vector.tensor_scalar(gain_zz[:], gains[:], neg_rz[:], neg_rz[:], ALU.mult, ALU.mult)

        su = sb.tile([P, I], F32, name="su")
        su_sum = col("su_sum")
        nc.vector.scalar_tensor_tensor(su[:], px[:], mult_sb[:], sw_all[:], ALU.mult, ALU.mult, accum_out=su_sum[:])
        w = sb.tile([P, I], F32, name="w")
        w_sum = col("w_sum")
        nc.vector.scalar_tensor_tensor(w[:], a_l[:], shift[:], su[:], ALU.add, ALU.mult, accum_out=w_sum[:])
        ta_l = su
        nc.vector.tensor_copy(ta_l[:], ta[:].indirect(offsets[:]))
        xe = sb.tile([P, I], F32, name="xe")
        xe_sum = col("xe_sum")
        nc.vector.scalar_tensor_tensor(xe[:], ta_l[:], neg_mean[:], w[:], ALU.add, ALU.mult, accum_out=xe_sum[:])
        nc.vector.tensor_copy(xs[:].indirect(offsets[:]), xe[:])

        gain_z = col("gain_z")
        nc.scalar.activation(gain_z[:], neg_rz[:], ACT.Identity, scale=GAIN)
        sw_term = col("sw_term")
        nc.scalar.activation(sw_scaled[:], sw_all[:], ACT.Identity, scale=gain_z[:], accum_out=sw_term[:])
        dz_part = col("dz_part")
        nc.scalar.activation(dz_part[:], su_sum[:], ACT.Identity, scale=gain_zz[:, 0:1], bias=sw_term[:])
        xp_fac = col("xp_fac")
        nc.scalar.activation(xp_fac[:], w_sum[:], ACT.Identity, scale=gain_zz[:, 1:2], bias=dz_part[:])
        mean_term = col("mean_term")
        nc.scalar.activation(mean_term[:], xp_fac[:], ACT.Identity, scale=neg_mean[:])

        def base_cols(c):
            return base_sb[c // 2][:, (c % 2) * N : (c % 2 + 1) * N]

        def finish(c, dense, pieces):
            width = N // pieces
            for k in range(pieces):
                inside = slice(k * width, (k + 1) * width)
                cols = slice(c * N + k * width, c * N + (k + 1) * width)
                res = sb.tile([P, width], F32, name="res%d_%d" % (c, k))
                nc.vector.scalar_tensor_tensor(res[:], xs[:, cols], gain_z[:], dense[:, inside], ALU.mult, ALU.add)
                nc.sync.dma_start(out=out[:, cols], in_=res[:])

        def turn(bank, term, start, stop):
            for b in range(BLOCKS):
                blk = slice(b * P, (b + 1) * P)
                nc.tensor.matmul(
                    bank[:, blk],
                    lhsT=term[:, blk],
                    rhs=ident[:],
                    is_transpose=True,
                    start=start and b == 0,
                    stop=stop and b == BLOCKS - 1,
                )

        ta_fac_first = col("ta_fac_first")
        nc.scalar.activation(ta_fac_first[:], xp_fac[:], ACT.Identity, scale=rescale[:])
        mean_term_first = col("mean_term_first")
        nc.scalar.activation(mean_term_first[:], mean_term[:], ACT.Identity, scale=rescale[:])
        gain_zz_first = col("gain_zz_first")
        nc.scalar.activation(gain_zz_first[:], gain_zz[:, 1:2], ACT.Identity, scale=rescale[:])

        turned = range(1, CHUNKS)
        sum_ps = {c: ps.tile([P, N], F32, name="sum_ps%d" % c, tag="bank%d" % c) for c in turned}
        for c in turned:
            turn(sum_ps[c], base_cols(c), True, False)
        for c in turned:
            xp_term = sb.tile([P, N], F32, name="xp_term%d" % c)
            nc.scalar.activation(xp_term[:], xp[:, chunk[c]], ACT.Identity, scale=xp_fac[:])
            turn(sum_ps[c], xp_term, False, False)
        p_fac_first = col("p_fac_first")
        nc.scalar.activation(p_fac_first[:], xe_sum[:], ACT.Identity, scale=gain_zz_first[:], bias=mean_term_first[:])
        p_fac = col("p_fac")
        nc.scalar.activation(p_fac[:], xe_sum[:], ACT.Identity, scale=gain_zz[:, 1:2], bias=mean_term[:])

        slope = sb.tile([P, N], F32, name="slope")
        nc.gpsimd.tensor_scalar(slope[:], ta[:, first], ta_fac_first[:], p_fac_first[:], ALU.mult, ALU.add)
        spread = sb.tile([P, N], F32, name="spread")
        nc.gpsimd.tensor_tensor(spread[:], slope[:], p[:, first], ALU.mult)
        dense_first = sb.tile([P, N], F32, name="dense_first")
        nc.vector.tensor_tensor(dense_first[:], spread[:], base_cols(0), ALU.add)
        finish(0, dense_first, 1)

        for c in turned:
            p_term = sb.tile([P, N], F32, name="p_term%d" % c)
            nc.scalar.activation(p_term[:], p[:, chunk[c]], ACT.Identity, scale=p_fac[:])
            turn(sum_ps[c], p_term, False, True)
        for c in turned:
            sum_sb = sb.tile([P, N], F32, name="sum_sb%d" % c)
            nc.scalar.copy(sum_sb[:], sum_ps[c][:])
            dense_ps = ps.tile([P, N], F32, name="dense_ps%d" % c, tag="bank%d" % (CHUNKS + c))
            for b in range(BLOCKS):
                blk = slice(b * P, (b + 1) * P)
                nc.tensor.transpose(dense_ps[:, blk], sum_sb[:, blk], ident[:])
            finish(c, dense_ps, LAST_PIECES if c == CHUNKS - 1 else 1)
